import numpy as np
import ml_dtypes


def mxq(x, axis, fmt="e4m3"):
    dtype, down = {"e4m3": (ml_dtypes.float8_e4m3fn, 7), "e5m2": (ml_dtypes.float8_e5m2, 14)}[fmt]
    v = np.moveaxis(np.asarray(x, np.float32).astype(ml_dtypes.bfloat16).astype(np.float64), axis, -1)
    blocks = v.reshape(v.shape[:-1] + (-1, 32))
    amax = np.abs(blocks).max(-1, keepdims=True)
    byte = np.maximum(np.where(amax > 0, np.frexp(amax)[1] - 1 + 127, 0) - down, 1)
    scale = np.exp2(byte - 127.0)
    codes = (blocks / scale).astype(np.float32).astype(dtype).astype(np.float64)
    return np.moveaxis((codes * scale).reshape(v.shape), -1, axis)


WIDE = False


def mx_kscale(k):
    if not WIDE:
        return np.ones(k)
    levels = np.array([10, -10, 5, -5, 0])
    if k % 512:
        return np.exp2(np.random.permutation(np.resize(levels, k // 32))).repeat(32)
    a = np.empty((k // 512, 16))
    for p in range(k // 512):
        a[p, :8] = np.random.permutation(np.resize(levels, 8))
        for g in range(8):
            far = levels[np.abs(levels - a[p, g]) >= 10]
            a[p, g + 8] = far[np.random.randint(len(far))]
    return np.exp2(a.ravel()).repeat(32)


def f64(x):
    return np.asarray(x).astype(np.float64)


def striped(idx):
    return np.tile(idx.reshape(-1, 16).T, (8, 1)).astype(np.uint16)


def unstriped(offs):
    return offs[:16].T.reshape(-1).astype(np.int64)


def pack_weight(w):
    k, n = w.shape
    w = f64(np.asarray(w, np.float32).astype(ml_dtypes.bfloat16)).reshape(k // 32, 32, n)
    amax = np.abs(w).max(1)
    byte = np.clip(np.where(amax > 0, np.frexp(amax)[1] - 1 + 127 - 7, 1), 1, 254)
    scaled = (w * np.exp2(127.0 - byte)[:, None, :]).reshape(k, n).astype(np.float32)
    words = np.ascontiguousarray(scaled.reshape(k // 512, 128, 4, n).transpose(0, 1, 3, 2)).astype(ml_dtypes.float8_e4m3fn).view(np.uint8)
    return words, np.ascontiguousarray(byte.astype(np.uint8).reshape(k // 512, 16, n))


def unpack_weight(words, scales):
    g, p, n, _ = words.shape
    vals = np.ascontiguousarray(words).view(ml_dtypes.float8_e4m3fn).astype(np.float64) * np.repeat(np.exp2(scales.astype(np.float64) - 127.0), 8, axis=1)[..., None]
    return vals.transpose(0, 1, 3, 2).reshape(g * 512, n)


K, T, S, D, N, V = 1024, 2048, 1024, 2, 256, 512


def setup_inputs():
    n = np.random.standard_normal
    s = mx_kscale(K)[:, None]
    packed_xT = pack_weight(n((K, T)) * s)
    return {
        "x_words": packed_xT[0],
        "x_scales": packed_xT[1],
        "w1": (n((K, N)) / np.sqrt(K) / s).astype(np.float32),
        "w2": (n((K, N)) / np.sqrt(K) / s).astype(np.float32),
        "w3": (n((K, N)) / np.sqrt(K) / s).astype(np.float32),
        "w4": (n((K, N)) / np.sqrt(K) / s).astype(np.float32),
        "offs": striped(np.random.permutation(T)[:S]),
        "parent": striped(np.random.permutation(T)[:V]),
    }


def reference(x_words, x_scales, w1, w2, w3, w4, offs, parent):
    xq = unpack_weight(x_words, x_scales)[:, unstriped(offs)]
    y = mxq(f64(w1), 0, "e4m3").T @ xq
    va = np.exp(mxq(f64(w2), 0, "e4m3").T @ xq)
    x_parent = unpack_weight(x_words, x_scales)[:, unstriped(parent)]
    h = mxq(f64(w3), 0, "e4m3").T @ x_parent
    wv = np.exp(mxq(f64(w4), 0, "e4m3").T @ x_parent)
    gg = (h - (y.reshape(len(y), -1, D).sum(axis=2))) / (wv + va.reshape(len(va), -1, D).sum(axis=2))
    return y + va * np.repeat(gg, D, axis=1)

@@ -1,0 +1,228 @@
+from contextlib import ExitStack
+
+import concourse.mybir as mybir
+from concourse.masks import make_identity
+
+F32 = mybir.dt.float32
+BF16 = mybir.dt.bfloat16
+I32 = mybir.dt.int32
+U32 = mybir.dt.uint32
+U16 = mybir.dt.uint16
+U8 = mybir.dt.uint8
+FP8X4 = mybir.dt.float8_e4m3fn_x4
+ACT = mybir.ActivationFunctionType
+ALU = mybir.AluOpType
+
+P = 128
+PACK = 4
+K_PASS = P * PACK
+PASSES = 2
+T = 2048
+LEAVES = 1024
+PARENTS = 512
+M = 256
+M_TILES = M // P
+HALVES = 2
+HL = LEAVES // HALVES
+HP = PARENTS // HALVES
+FLOPS = 2 * 1024 * M * (2 * LEAVES + 2 * PARENTS)
+
+
+def tile_picked_yrecon_leaf_p_kernel(
+    tc, x_words, x_scales, w1, w2, w3, w4, offs, parent, out
+):
+    nc = tc.nc
+    with ExitStack() as ctx:
+        keep = ctx.enter_context(tc.tile_pool(name="keep", bufs=1))
+        psum = ctx.enter_context(tc.psum_pool(name="psum", bufs=1))
+
+        leaf_list = keep.tile([P, LEAVES // 16], U16, name="leaf_list")
+        parent_list = keep.tile([P, PARENTS // 16], U16, name="parent_list")
+        scale_table = keep.tile([P, T], U8, name="scale_table", align_bytes=64)
+        word_table = [keep.tile([P, T], I32, name="word_table%d" % o, align_bytes=64) for o in range(PASSES)]
+
+        nc.gpsimd.memset(scale_table[:].bitcast(I32), 0)
+        nc.sync.dma_start(leaf_list[:], offs)
+
+        def load_words(o):
+            nc.sync.dma_start(word_table[o][:], x_words[o].rearrange("p c r -> p (c r)").bitcast(I32))
+
+        weights = {1: w1, 2: w2, 3: w3, 4: w4}
+        raw = {}
+
+        def load_weight(i, o):
+            raw[i, o] = keep.tile([P, PACK, M], F32, name="raw%d_%d" % (i, o))
+            rows = weights[i][o * K_PASS : (o + 1) * K_PASS, :]
+            nc.sync.dma_start(raw[i, o][:], rows.rearrange("(p j) m -> p j m", j=PACK))
+
+        load_words(0)
+        for q in range(4):
+            nc.sync.dma_start(
+                scale_table[32 * q : 32 * q + 4 * PASSES, :].bitcast(I32),
+                x_scales[:, 4 * q : 4 * q + 4, :].bitcast(I32),
+            )
+        nc.sync.dma_start(parent_list[:], parent)
+        early = ((4, 0), (2, 0), (4, 1), (2, 1), (1, 0), (1, 1))
+        for i, o in early:
+            load_weight(i, o)
+        load_words(1)
+        for o in range(PASSES):
+            load_weight(3, o)
+
+        ident = keep.tile([P, P], F32, name="ident")
+        make_identity(nc, ident[:])
+
+        grouped = {}
+        codes = {}
+        scales = {}
+
+        def interleave(i, o, copy):
+            grouped[i, o] = keep.tile([P, M, PACK], BF16, name="grouped%d_%d" % (i, o), align_bytes=64)
+            copy(
+                grouped[i, o][:].rearrange("p (c e) j -> p c j e", e=4),
+                raw[i, o][:].rearrange("p j (c e) -> p c j e", e=4),
+            )
+
+        def quantize(i, o):
+            codes[i, o] = keep.tile([P, M], U32, name="codes%d_%d" % (i, o), align_bytes=64)
+            scales[i, o] = keep.tile([P, M], U8, name="scales%d_%d" % (i, o), align_bytes=64)
+            nc.vector.quantize_mx(
+                out=codes[i, o][:].bitcast(FP8X4),
+                scales=scales[i, o][:],
+                in_=grouped[i, o][:].rearrange("p m j -> p (m j)"),
+            )
+
+        def gather(name, table, offsets, width, dtype):
+            picked = keep.tile([P, width], dtype, name=name, align_bytes=64)
+            nc.vector.tensor_copy(picked[:], table.indirect(offsets))
+            return picked
+
+        def product(bank, i, o, mt, x_codes, x_planes):
+            cols = slice(mt * P, (mt + 1) * P)
+            nc.tensor.matmul_mx(
+                out=bank,
+                lhsT=codes[i, o][:, cols].bitcast(FP8X4),
+                lhsT_scale=scales[i, o][:, cols],
+                rhs=x_codes.bitcast(FP8X4),
+                rhs_scale=x_planes,
+                start=(o == 0),
+                stop=(o == PASSES - 1),
+            )
+
+        leaf_words0 = gather("leaf_words0", word_table[0][:].bitcast(U32), leaf_list[:], LEAVES, U32)
+        parent_words = [gather("parent_words0", word_table[0][:].bitcast(U32), parent_list[:], PARENTS, U32)]
+        parent_scales = gather("parent_scales", scale_table[:], parent_list[:], PARENTS, U8)
+        leaf_scales = gather("leaf_scales", scale_table[:], leaf_list[:], LEAVES, U8)
+        for i, o in early:
+            interleave(i, o, nc.scalar.copy)
+            quantize(i, o)
+        parent_words.append(gather("parent_words1", word_table[1][:].bitcast(U32), parent_list[:], PARENTS, U32))
+        leaf_words = {}
+        for g in range(HALVES):
+            leaf_words[0, g] = leaf_words0[:, g * HL : (g + 1) * HL]
+            piece = leaf_list[:, g * HL // 16 : (g + 1) * HL // 16]
+            leaf_words[1, g] = gather("leaf_words1_%d" % g, word_table[1][:].bitcast(U32), piece, HL, U32)[:]
+
+        def leaf_product(bank, i, mt, g):
+            for o in range(PASSES):
+                product(bank, i, o, mt, leaf_words[o, g], leaf_scales[4 * o : P, g * HL : (g + 1) * HL])
+
+        def parent_product(bank, i, mt):
+            for o in range(PASSES):
+                product(bank, i, o, mt, parent_words[o][:], parent_scales[4 * o : P, :])
+
+        wv = []
+        den_t = []
+        for mt in range(M_TILES):
+            bank = psum.tile([P, PARENTS], F32, name="log_wv%d" % mt, tag="a%d" % mt)
+            parent_product(bank[:], 4, mt)
+            wv.append(keep.tile([P, PARENTS], F32, name="wv%d" % mt))
+            nc.scalar.activation(wv[mt][:], bank[:], ACT.Exp)
+        for mt in range(M_TILES):
+            den_t.append(psum.tile([P, PARENTS // P, P], F32, name="den_t%d" % mt, tag="turn%d" % mt))
+            for block in range(PARENTS // P):
+                term = wv[mt][:, block * P : (block + 1) * P]
+                nc.tensor.matmul(den_t[mt][:, block, :], term, ident[:], start=(block == 0), stop=False, is_transpose=True)
+        va = {}
+        y = {}
+        for g in range(HALVES):
+            for mt in range(M_TILES):
+                bank = psum.tile([P, HL], F32, name="log_va%d_%d" % (mt, g), tag="bc"[g] + str(mt))
+                leaf_product(bank[:], 2, mt, g)
+                va[mt, g] = keep.tile([P, 2, HP], F32, name="va%d_%d" % (mt, g))
+                nc.scalar.activation(va[mt, g][:], bank[:].rearrange("p (v d) -> p d v", d=2), ACT.Exp)
+        for g in range(HALVES):
+            for mt in range(M_TILES):
+                for b in range(HP // P):
+                    for d in range(2):
+                        last = g == HALVES - 1 and b == HP // P - 1 and d == 1
+                        nc.tensor.matmul(
+                            den_t[mt][:, g * (HP // P) + b, :],
+                            va[mt, g][:, d, b * P : (b + 1) * P],
+                            ident[:],
+                            start=False,
+                            stop=last,
+                            is_transpose=True,
+                        )
+            for mt in range(M_TILES):
+                y[mt, g] = psum.tile([P, HL], F32, name="y%d_%d" % (mt, g), tag="ab"[g] + str(mt))
+                leaf_product(y[mt, g][:], 1, mt, g)
+
+        interleave(3, 0, nc.vector.tensor_copy)
+        interleave(3, 1, nc.vector.tensor_copy)
+        quantize(3, 0)
+        quantize(3, 1)
+        h = []
+        for mt in range(M_TILES):
+            h.append(psum.tile([P, PARENTS], F32, name="h%d" % mt, tag="c%d" % mt))
+            parent_product(h[mt][:], 3, mt)
+
+        inverse = []
+        for mt in range(M_TILES):
+            root_t = keep.tile([P, PARENTS], F32, name="root_t%d" % mt)
+            nc.scalar.activation(root_t[:], den_t[mt][:].rearrange("p b m -> p (b m)"), ACT.Abs_reciprocal_sqrt)
+            inverse_t = keep.tile([P, PARENTS], F32, name="inverse_t%d" % mt)
+            nc.scalar.activation(inverse_t[:], root_t[:], ACT.Square)
+            inverse.append(psum.tile([P, PARENTS], F32, name="inverse%d" % mt, tag="turn%d" % mt))
+            for block in range(PARENTS // P):
+                cols = slice(block * P, (block + 1) * P)
+                nc.tensor.transpose(inverse[mt][:, cols], inverse_t[:, cols], ident[:])
+
+        pair_sum = [keep.tile([P, PARENTS], F32, name="pair_sum%d" % mt) for mt in range(M_TILES)]
+        for g in range(HALVES):
+            for mt in range(M_TILES):
+                nc.vector.tensor_reduce(
+                    pair_sum[mt][:, g * HP : (g + 1) * HP],
+                    y[mt, g][:].rearrange("p (v d) -> p v d", d=2),
+                    mybir.AxisListType.X,
+                    ALU.add,
+                )
+        gap = []
+        for mt in range(M_TILES):
+            gap.append(keep.tile([P, PARENTS], F32, name="gap%d" % mt))
+            nc.vector.tensor_tensor(gap[mt][:], h[mt][:], pair_sum[mt][:], ALU.subtract)
+        gg = []
+        for mt in range(M_TILES):
+            gg.append(keep.tile([P, PARENTS], F32, name="gg%d" % mt))
+            nc.vector.tensor_tensor(gg[mt][:], inverse[mt][:], gap[mt][:], ALU.mult)
+        for mt in range(M_TILES):
+            share = []
+            for g in range(HALVES):
+                share.append(keep.tile([P, 2, HP], F32, name="share%d_%d" % (mt, g)))
+                nc.vector.tensor_tensor(
+                    share[g][:],
+                    va[mt, g][:],
+                    gg[mt][:, g * HP : (g + 1) * HP].unsqueeze(1).to_broadcast([P, 2, HP]),
+                    ALU.mult,
+                )
+            for g in range(HALVES):
+                result = keep.tile([P, HP, 2], F32, name="result%d_%d" % (mt, g))
+                nc.vector.tensor_tensor(
+                    result[:],
+                    y[mt, g][:].rearrange("p (v d) -> p v d", d=2),
+                    share[g][:].rearrange("p d v -> p v d"),
+                    ALU.add,
+                )
+                nc.sync.dma_start(
+                    out[mt * P : (mt + 1) * P, g * HL : (g + 1) * HL], result[:].rearrange("p v d -> p (v d)")
+                )

@@ -1,7 +1,6 @@
 from contextlib import ExitStack
 
 import concourse.mybir as mybir
-from concourse.masks import make_identity
 
 F32 = mybir.dt.float32
 BF16 = mybir.dt.bfloat16
@@ -25,6 +24,7 @@ M_TILES = M // P
 HALVES = 2
 HL = LEAVES // HALVES
 HP = PARENTS // HALVES
+PIECE = 256
 FLOPS = 2 * 1024 * M * (2 * LEAVES + 2 * PARENTS)
 
 
@@ -51,26 +51,24 @@ def tile_picked_yrecon_leaf_p_kernel(
         raw = {}
 
         def load_weight(i, o):
-            raw[i, o] = keep.tile([P, PACK, M], F32, name="raw%d_%d" % (i, o))
+            raw[i, o] = keep.tile([P, PACK, M], F32, name="raw%d_%d" % (i, o), tag="raw%d_%d" % (i, o))
             rows = weights[i][o * K_PASS : (o + 1) * K_PASS, :]
             nc.sync.dma_start(raw[i, o][:], rows.rearrange("(p j) m -> p j m", j=PACK))
 
-        load_words(0)
+        nc.sync.dma_start(parent_list[:], parent)
         for q in range(4):
             nc.sync.dma_start(
                 scale_table[32 * q : 32 * q + 4 * PASSES, :].bitcast(I32),
                 x_scales[:, 4 * q : 4 * q + 4, :].bitcast(I32),
             )
-        nc.sync.dma_start(parent_list[:], parent)
-        early = ((4, 0), (2, 0), (4, 1), (2, 1), (1, 0), (1, 1))
+        load_words(0)
+        early = ((4, 0), (2, 0), (4, 1), (2, 1))
         for i, o in early:
             load_weight(i, o)
         load_words(1)
-        for o in range(PASSES):
-            load_weight(3, o)
-
-        ident = keep.tile([P, P], F32, name="ident")
-        make_identity(nc, ident[:])
+        for i in (1, 3):
+            for o in range(PASSES):
+                load_weight(i, o)
 
         grouped = {}
         codes = {}
@@ -97,7 +95,7 @@ def tile_picked_yrecon_leaf_p_kernel(
             nc.vector.tensor_copy(picked[:], table.indirect(offsets))
             return picked
 
-        def product(bank, i, o, mt, x_codes, x_planes):
+        def product(bank, i, o, mt, x_codes, x_planes, start, stop):
             cols = slice(mt * P, (mt + 1) * P)
             nc.tensor.matmul_mx(
                 out=bank,
@@ -105,124 +103,122 @@ def tile_picked_yrecon_leaf_p_kernel(
                 lhsT_scale=scales[i, o][:, cols],
                 rhs=x_codes.bitcast(FP8X4),
                 rhs_scale=x_planes,
-                start=(o == 0),
-                stop=(o == PASSES - 1),
+                start=start,
+                stop=stop,
             )
 
-        leaf_words0 = gather("leaf_words0", word_table[0][:].bitcast(U32), leaf_list[:], LEAVES, U32)
-        parent_words = [gather("parent_words0", word_table[0][:].bitcast(U32), parent_list[:], PARENTS, U32)]
-        parent_scales = gather("parent_scales", scale_table[:], parent_list[:], PARENTS, U8)
         leaf_scales = gather("leaf_scales", scale_table[:], leaf_list[:], LEAVES, U8)
+        parent_scales = gather("parent_scales", scale_table[:], parent_list[:], PARENTS, U8)
+        leaf_words0 = gather("leaf_words0", word_table[0][:].bitcast(U32), leaf_list[:], LEAVES, U32)
+        parent_words0 = gather("parent_words0", word_table[0][:].bitcast(U32), parent_list[:], PARENTS, U32)
         for i, o in early:
             interleave(i, o, nc.scalar.copy)
             quantize(i, o)
-        parent_words.append(gather("parent_words1", word_table[1][:].bitcast(U32), parent_list[:], PARENTS, U32))
-        leaf_words = {}
-        for g in range(HALVES):
-            leaf_words[0, g] = leaf_words0[:, g * HL : (g + 1) * HL]
-            piece = leaf_list[:, g * HL // 16 : (g + 1) * HL // 16]
-            leaf_words[1, g] = gather("leaf_words1_%d" % g, word_table[1][:].bitcast(U32), piece, HL, U32)[:]
+        for o in range(PASSES):
+            interleave(1, o, nc.scalar.copy)
 
-        def leaf_product(bank, i, mt, g):
+        leaf_words1 = keep.tile([P, LEAVES], U32, name="leaf_words1", align_bytes=64)
+        parent_words1 = keep.tile([P, PARENTS], U32, name="parent_words1", align_bytes=64)
+        leaf_side = (leaf_list, (leaf_words0, leaf_words1), leaf_scales)
+        parent_side = (parent_list, (parent_words0, parent_words1), parent_scales)
+
+        def both_tiles(bank, i, side, cols):
             for o in range(PASSES):
-                product(bank, i, o, mt, leaf_words[o, g], leaf_scales[4 * o : P, g * HL : (g + 1) * HL])
+                for mt in range(M_TILES):
+                    first = o == 0 and mt == 0
+                    last = o == PASSES - 1 and mt == M_TILES - 1
+                    product(bank[:, mt, :], i, o, mt, side[1][o][:, cols], side[2][4 * o : P, cols], first, last)
 
-        def parent_product(bank, i, mt):
-            for o in range(PASSES):
-                product(bank, i, o, mt, parent_words[o][:], parent_scales[4 * o : P, :])
+        def log_variance(name, i, side, n, tag):
+            cols = slice(n * PIECE, (n + 1) * PIECE)
+            offsets = side[0][:, n * PIECE // 16 : (n + 1) * PIECE // 16]
+            nc.vector.tensor_copy(side[1][1][:, cols], word_table[1][:].bitcast(U32).indirect(offsets))
+            bank = psum.tile([P, M_TILES, PIECE], F32, name=name, tag=tag)
+            both_tiles(bank, i, side, cols)
+            return bank
 
-        wv = []
-        den_t = []
-        for mt in range(M_TILES):
-            bank = psum.tile([P, PARENTS], F32, name="log_wv%d" % mt, tag="a%d" % mt)
-            parent_product(bank[:], 4, mt)
-            wv.append(keep.tile([P, PARENTS], F32, name="wv%d" % mt))
-            nc.scalar.activation(wv[mt][:], bank[:], ACT.Exp)
-        for mt in range(M_TILES):
-            den_t.append(psum.tile([P, PARENTS // P, P], F32, name="den_t%d" % mt, tag="turn%d" % mt))
-            for block in range(PARENTS // P):
-                term = wv[mt][:, block * P : (block + 1) * P]
-                nc.tensor.matmul(den_t[mt][:, block, :], term, ident[:], start=(block == 0), stop=False, is_transpose=True)
-        va = {}
+        def leaf_pass(mt, g, o):
+            cols = slice(g * HL, (g + 1) * HL)
+            product(y[mt, g][:], 1, o, mt, leaf_side[1][o][:, cols], leaf_scales[4 * o : P, cols], o == 0, o == PASSES - 1)
+
+        blocks = HP // P
         y = {}
+        variances = keep.tile([P, M_TILES * (PARENTS + LEAVES)], F32, name="variances", tag="raw1_1")
+        wv = []
+        va = []
         for g in range(HALVES):
-            for mt in range(M_TILES):
-                bank = psum.tile([P, HL], F32, name="log_va%d_%d" % (mt, g), tag="bc"[g] + str(mt))
-                leaf_product(bank[:], 2, mt, g)
-                va[mt, g] = keep.tile([P, 2, HP], F32, name="va%d_%d" % (mt, g))
-                nc.scalar.activation(va[mt, g][:], bank[:].rearrange("p (v d) -> p d v", d=2), ACT.Exp)
-        for g in range(HALVES):
-            for mt in range(M_TILES):
-                for b in range(HP // P):
-                    for d in range(2):
-                        last = g == HALVES - 1 and b == HP // P - 1 and d == 1
-                        nc.tensor.matmul(
-                            den_t[mt][:, g * (HP // P) + b, :],
-                            va[mt, g][:, d, b * P : (b + 1) * P],
-                            ident[:],
-                            start=False,
-                            stop=last,
-                            is_transpose=True,
-                        )
-            for mt in range(M_TILES):
-                y[mt, g] = psum.tile([P, HL], F32, name="y%d_%d" % (mt, g), tag="ab"[g] + str(mt))
-                leaf_product(y[mt, g][:], 1, mt, g)
+            first = g * M_TILES * (HP + HL)
+            middle = first + M_TILES * HP
+            wv.append(variances[:, first:middle].rearrange("p (t v) -> p t v", t=M_TILES))
+            va.append(variances[:, middle : middle + M_TILES * HL].rearrange("p (t j) -> p t j", t=M_TILES))
 
-        interleave(3, 0, nc.vector.tensor_copy)
-        interleave(3, 1, nc.vector.tensor_copy)
-        quantize(3, 0)
-        quantize(3, 1)
+        def parent_piece(g):
+            bank = log_variance("log_wv%d" % g, 4, parent_side, g, "bank%d" % (5 * g))
+            nc.scalar.activation(wv[g], bank[:], ACT.Exp)
+
+        def leaf_piece(n):
+            bank = log_variance("log_va%d" % n, 2, leaf_side, n, "bank%d" % (n + 1))
+            b = n % blocks
+            nc.scalar.activation(va[n // blocks][:, :, b * PIECE : (b + 1) * PIECE], bank[:], ACT.Exp)
+
+        parent_piece(0)
+        for n in range(LEAVES // PIECE):
+            leaf_piece(n)
+        parent_piece(1)
+        for o in range(PASSES):
+            quantize(1, o)
+        for g in range(HALVES):
+            for mt in range(M_TILES):
+                y[mt, g] = psum.tile([P, HL], F32, name="y%d_%d" % (mt, g), tag="bank%d" % ((6 + 2 * g + mt) % 8))
+                for o in range(PASSES):
+                    leaf_pass(mt, g, o)
+
+        den = []
+
+        def denominator(g):
+            both = keep.tile([P, M_TILES, HP], F32, name="both%d" % g)
+            nc.vector.tensor_tensor(both[:], va[g][:, :, 0:HL:2], va[g][:, :, 1:HL:2], ALU.add)
+            den.append(keep.tile([P, M_TILES, HP], F32, name="den%d" % g))
+            nc.vector.tensor_tensor(den[g][:], both[:], wv[g], ALU.add)
+
+        for g in range(HALVES):
+            interleave(3, g, nc.vector.tensor_copy)
+            denominator(g)
+            quantize(3, g)
         h = []
-        for mt in range(M_TILES):
-            h.append(psum.tile([P, PARENTS], F32, name="h%d" % mt, tag="c%d" % mt))
-            parent_product(h[mt][:], 3, mt)
-
-        inverse = []
-        for mt in range(M_TILES):
-            root_t = keep.tile([P, PARENTS], F32, name="root_t%d" % mt)
-            nc.scalar.activation(root_t[:], den_t[mt][:].rearrange("p b m -> p (b m)"), ACT.Abs_reciprocal_sqrt)
-            inverse_t = keep.tile([P, PARENTS], F32, name="inverse_t%d" % mt)
-            nc.scalar.activation(inverse_t[:], root_t[:], ACT.Square)
-            inverse.append(psum.tile([P, PARENTS], F32, name="inverse%d" % mt, tag="turn%d" % mt))
-            for block in range(PARENTS // P):
-                cols = slice(block * P, (block + 1) * P)
-                nc.tensor.transpose(inverse[mt][:, cols], inverse_t[:, cols], ident[:])
-
-        pair_sum = [keep.tile([P, PARENTS], F32, name="pair_sum%d" % mt) for mt in range(M_TILES)]
         for g in range(HALVES):
-            for mt in range(M_TILES):
-                nc.vector.tensor_reduce(
-                    pair_sum[mt][:, g * HP : (g + 1) * HP],
-                    y[mt, g][:].rearrange("p (v d) -> p v d", d=2),
-                    mybir.AxisListType.X,
-                    ALU.add,
-                )
+            h.append(psum.tile([P, M_TILES, HP], F32, name="h%d" % g, tag="bank%d" % (2 + g)))
+            both_tiles(h[g], 3, parent_side, slice(g * HP, (g + 1) * HP))
+
         gap = []
-        for mt in range(M_TILES):
-            gap.append(keep.tile([P, PARENTS], F32, name="gap%d" % mt))
-            nc.vector.tensor_tensor(gap[mt][:], h[mt][:], pair_sum[mt][:], ALU.subtract)
-        gg = []
-        for mt in range(M_TILES):
-            gg.append(keep.tile([P, PARENTS], F32, name="gg%d" % mt))
-            nc.vector.tensor_tensor(gg[mt][:], inverse[mt][:], gap[mt][:], ALU.mult)
-        for mt in range(M_TILES):
+        inverse = []
+        for g in range(HALVES):
+            odd = keep.tile([P, M_TILES, HP], F32, name="odd%d" % g)
+            pair_sum = keep.tile([P, M_TILES, HP], F32, name="pair_sum%d" % g)
+            for mt in range(M_TILES):
+                nc.scalar.copy(odd[:, mt, :], y[mt, g][:, 1:HL:2])
+                nc.vector.tensor_tensor(pair_sum[:, mt, :], y[mt, g][:, 0:HL:2], odd[:, mt, :], ALU.add)
+            gap.append(keep.tile([P, M_TILES, HP], F32, name="gap%d" % g))
+            nc.vector.tensor_tensor(gap[g][:], h[g][:], pair_sum[:], ALU.subtract)
+            root = keep.tile([P, M_TILES, HP], F32, name="root%d" % g)
+            nc.scalar.activation(root[:], den[g][:], ACT.Abs_reciprocal_sqrt)
+            inverse.append(keep.tile([P, M_TILES, HP], F32, name="inverse%d" % g))
+            nc.scalar.activation(inverse[g][:], root[:], ACT.Square)
+        for g in range(HALVES):
+            gg = []
+            for mt in range(M_TILES):
+                gg.append(keep.tile([P, HP], F32, name="gg%d_%d" % (mt, g)))
+                nc.vector.tensor_tensor(gg[mt][:], inverse[g][:, mt, :], gap[g][:, mt, :], ALU.mult)
             share = []
-            for g in range(HALVES):
-                share.append(keep.tile([P, 2, HP], F32, name="share%d_%d" % (mt, g)))
+            for mt in range(M_TILES):
+                share.append(keep.tile([P, HP, 2], F32, name="share%d_%d" % (mt, g)))
                 nc.vector.tensor_tensor(
-                    share[g][:],
-                    va[mt, g][:],
-                    gg[mt][:, g * HP : (g + 1) * HP].unsqueeze(1).to_broadcast([P, 2, HP]),
+                    share[mt][:],
+                    va[g][:, mt, :].rearrange("p (v d) -> p v d", d=2),
+                    gg[mt][:].unsqueeze(2).to_broadcast([P, HP, 2]),
                     ALU.mult,
                 )
-            for g in range(HALVES):
-                result = keep.tile([P, HP, 2], F32, name="result%d_%d" % (mt, g))
-                nc.vector.tensor_tensor(
-                    result[:],
-                    y[mt, g][:].rearrange("p (v d) -> p v d", d=2),
-                    share[g][:].rearrange("p d v -> p v d"),
-                    ALU.add,
-                )
-                nc.sync.dma_start(
-                    out[mt * P : (mt + 1) * P, g * HL : (g + 1) * HL], result[:].rearrange("p v d -> p (v d)")
-                )
+            for mt in range(M_TILES):
+                result = keep.tile([P, HL], F32, name="result%d_%d" % (mt, g))
+                nc.vector.tensor_tensor(result[:], y[mt, g][:], share[mt][:].rearrange("p v d -> p (v d)"), ALU.add)
+                nc.sync.dma_start(out[mt * P : (mt + 1) * P, g * HL : (g + 1) * HL], result[:])

from contextlib import ExitStack

import concourse.mybir as mybir

F32 = mybir.dt.float32
BF16 = mybir.dt.bfloat16
I32 = mybir.dt.int32
U32 = mybir.dt.uint32
U16 = mybir.dt.uint16
U8 = mybir.dt.uint8
FP8X4 = mybir.dt.float8_e4m3fn_x4
ACT = mybir.ActivationFunctionType
ALU = mybir.AluOpType

P = 128
PACK = 4
K_PASS = P * PACK
PASSES = 2
T = 2048
LEAVES = 1024
PARENTS = 512
M = 256
M_TILES = M // P
HALVES = 2
HL = LEAVES // HALVES
HP = PARENTS // HALVES
PIECE = 256
FLOPS = 2 * 1024 * M * (2 * LEAVES + 2 * PARENTS)


def tile_picked_yrecon_leaf_p_kernel(
    tc, x_words, x_scales, w1, w2, w3, w4, offs, parent, out
):
    nc = tc.nc
    with ExitStack() as ctx:
        keep = ctx.enter_context(tc.tile_pool(name="keep", bufs=1))
        psum = ctx.enter_context(tc.psum_pool(name="psum", bufs=1))

        leaf_list = keep.tile([P, LEAVES // 16], U16, name="leaf_list")
        parent_list = keep.tile([P, PARENTS // 16], U16, name="parent_list")
        scale_table = keep.tile([P, T], U8, name="scale_table", align_bytes=64)
        word_table = [keep.tile([P, T], I32, name="word_table%d" % o, align_bytes=64) for o in range(PASSES)]

        nc.gpsimd.memset(scale_table[:].bitcast(I32), 0)
        nc.sync.dma_start(leaf_list[:], offs)

        def load_words(o):
            nc.sync.dma_start(word_table[o][:], x_words[o].rearrange("p c r -> p (c r)").bitcast(I32))

        weights = {1: w1, 2: w2, 3: w3, 4: w4}
        raw = {}

        def load_weight(i, o):
            raw[i, o] = keep.tile([P, PACK, M], F32, name="raw%d_%d" % (i, o), tag="raw%d_%d" % (i, o))
            rows = weights[i][o * K_PASS : (o + 1) * K_PASS, :]
            nc.sync.dma_start(raw[i, o][:], rows.rearrange("(p j) m -> p j m", j=PACK))

        nc.sync.dma_start(parent_list[:], parent)
        for q in range(4):
            nc.sync.dma_start(
                scale_table[32 * q : 32 * q + 4 * PASSES, :].bitcast(I32),
                x_scales[:, 4 * q : 4 * q + 4, :].bitcast(I32),
            )
        load_words(0)
        early = ((4, 0), (2, 0), (4, 1), (2, 1))
        for i, o in early:
            load_weight(i, o)
        load_words(1)
        for i in (1, 3):
            for o in range(PASSES):
                load_weight(i, o)

        grouped = {}
        codes = {}
        scales = {}

        def interleave(i, o, copy):
            grouped[i, o] = keep.tile([P, M, PACK], BF16, name="grouped%d_%d" % (i, o), align_bytes=64)
            copy(
                grouped[i, o][:].rearrange("p (c e) j -> p c j e", e=4),
                raw[i, o][:].rearrange("p j (c e) -> p c j e", e=4),
            )

        def quantize(i, o):
            codes[i, o] = keep.tile([P, M], U32, name="codes%d_%d" % (i, o), align_bytes=64)
            scales[i, o] = keep.tile([P, M], U8, name="scales%d_%d" % (i, o), align_bytes=64)
            nc.vector.quantize_mx(
                out=codes[i, o][:].bitcast(FP8X4),
                scales=scales[i, o][:],
                in_=grouped[i, o][:].rearrange("p m j -> p (m j)"),
            )

        def gather(name, table, offsets, width, dtype):
            picked = keep.tile([P, width], dtype, name=name, align_bytes=64)
            nc.vector.tensor_copy(picked[:], table.indirect(offsets))
            return picked

        def product(bank, i, o, mt, x_codes, x_planes, start, stop):
            cols = slice(mt * P, (mt + 1) * P)
            nc.tensor.matmul_mx(
                out=bank,
                lhsT=codes[i, o][:, cols].bitcast(FP8X4),
                lhsT_scale=scales[i, o][:, cols],
                rhs=x_codes.bitcast(FP8X4),
                rhs_scale=x_planes,
                start=start,
                stop=stop,
            )

        leaf_scales = gather("leaf_scales", scale_table[:], leaf_list[:], LEAVES, U8)
        parent_scales = gather("parent_scales", scale_table[:], parent_list[:], PARENTS, U8)
        leaf_words0 = gather("leaf_words0", word_table[0][:].bitcast(U32), leaf_list[:], LEAVES, U32)
        parent_words0 = gather("parent_words0", word_table[0][:].bitcast(U32), parent_list[:], PARENTS, U32)
        for i, o in early:
            interleave(i, o, nc.scalar.copy)
            quantize(i, o)
        for o in range(PASSES):
            interleave(1, o, nc.scalar.copy)

        leaf_words1 = keep.tile([P, LEAVES], U32, name="leaf_words1", align_bytes=64)
        parent_words1 = keep.tile([P, PARENTS], U32, name="parent_words1", align_bytes=64)
        leaf_side = (leaf_list, (leaf_words0, leaf_words1), leaf_scales)
        parent_side = (parent_list, (parent_words0, parent_words1), parent_scales)

        def both_tiles(bank, i, side, cols):
            for o in range(PASSES):
                for mt in range(M_TILES):
                    first = o == 0 and mt == 0
                    last = o == PASSES - 1 and mt == M_TILES - 1
                    product(bank[:, mt, :], i, o, mt, side[1][o][:, cols], side[2][4 * o : P, cols], first, last)

        def log_variance(name, i, side, n, tag):
            cols = slice(n * PIECE, (n + 1) * PIECE)
            offsets = side[0][:, n * PIECE // 16 : (n + 1) * PIECE // 16]
            nc.vector.tensor_copy(side[1][1][:, cols], word_table[1][:].bitcast(U32).indirect(offsets))
            bank = psum.tile([P, M_TILES, PIECE], F32, name=name, tag=tag)
            both_tiles(bank, i, side, cols)
            return bank

        def leaf_pass(mt, g, o):
            cols = slice(g * HL, (g + 1) * HL)
            product(y[mt, g][:], 1, o, mt, leaf_side[1][o][:, cols], leaf_scales[4 * o : P, cols], o == 0, o == PASSES - 1)

        blocks = HP // P
        y = {}
        variances = keep.tile([P, M_TILES * (PARENTS + LEAVES)], F32, name="variances", tag="raw1_1")
        wv = []
        va = []
        for g in range(HALVES):
            first = g * M_TILES * (HP + HL)
            middle = first + M_TILES * HP
            wv.append(variances[:, first:middle].rearrange("p (t v) -> p t v", t=M_TILES))
            va.append(variances[:, middle : middle + M_TILES * HL].rearrange("p (t j) -> p t j", t=M_TILES))

        def parent_piece(g):
            bank = log_variance("log_wv%d" % g, 4, parent_side, g, "bank%d" % (5 * g))
            nc.scalar.activation(wv[g], bank[:], ACT.Exp)

        def leaf_piece(n):
            bank = log_variance("log_va%d" % n, 2, leaf_side, n, "bank%d" % (n + 1))
            b = n % blocks
            nc.scalar.activation(va[n // blocks][:, :, b * PIECE : (b + 1) * PIECE], bank[:], ACT.Exp)

        parent_piece(0)
        for n in range(LEAVES // PIECE):
            leaf_piece(n)
        parent_piece(1)
        for o in range(PASSES):
            quantize(1, o)
        for g in range(HALVES):
            for mt in range(M_TILES):
                y[mt, g] = psum.tile([P, HL], F32, name="y%d_%d" % (mt, g), tag="bank%d" % ((6 + 2 * g + mt) % 8))
                for o in range(PASSES):
                    leaf_pass(mt, g, o)

        den = []

        def denominator(g):
            both = keep.tile([P, M_TILES, HP], F32, name="both%d" % g)
            nc.vector.tensor_tensor(both[:], va[g][:, :, 0:HL:2], va[g][:, :, 1:HL:2], ALU.add)
            den.append(keep.tile([P, M_TILES, HP], F32, name="den%d" % g))
            nc.vector.tensor_tensor(den[g][:], both[:], wv[g], ALU.add)

        for g in range(HALVES):
            interleave(3, g, nc.vector.tensor_copy)
            denominator(g)
            quantize(3, g)
        h = []
        for g in range(HALVES):
            h.append(psum.tile([P, M_TILES, HP], F32, name="h%d" % g, tag="bank%d" % (2 + g)))
            both_tiles(h[g], 3, parent_side, slice(g * HP, (g + 1) * HP))

        gap = []
        inverse = []
        for g in range(HALVES):
            odd = keep.tile([P, M_TILES, HP], F32, name="odd%d" % g)
            pair_sum = keep.tile([P, M_TILES, HP], F32, name="pair_sum%d" % g)
            for mt in range(M_TILES):
                nc.scalar.copy(odd[:, mt, :], y[mt, g][:, 1:HL:2])
                nc.vector.tensor_tensor(pair_sum[:, mt, :], y[mt, g][:, 0:HL:2], odd[:, mt, :], ALU.add)
            gap.append(keep.tile([P, M_TILES, HP], F32, name="gap%d" % g))
            nc.vector.tensor_tensor(gap[g][:], h[g][:], pair_sum[:], ALU.subtract)
            root = keep.tile([P, M_TILES, HP], F32, name="root%d" % g)
            nc.scalar.activation(root[:], den[g][:], ACT.Abs_reciprocal_sqrt)
            inverse.append(keep.tile([P, M_TILES, HP], F32, name="inverse%d" % g))
            nc.scalar.activation(inverse[g][:], root[:], ACT.Square)
        for g in range(HALVES):
            gg = []
            for mt in range(M_TILES):
                gg.append(keep.tile([P, HP], F32, name="gg%d_%d" % (mt, g)))
                nc.vector.tensor_tensor(gg[mt][:], inverse[g][:, mt, :], gap[g][:, mt, :], ALU.mult)
            share = []
            for mt in range(M_TILES):
                share.append(keep.tile([P, HP, 2], F32, name="share%d_%d" % (mt, g)))
                nc.vector.tensor_tensor(
                    share[mt][:],
                    va[g][:, mt, :].rearrange("p (v d) -> p v d", d=2),
                    gg[mt][:].unsqueeze(2).to_broadcast([P, HP, 2]),
                    ALU.mult,
                )
            for mt in range(M_TILES):
                result = keep.tile([P, HL], F32, name="result%d_%d" % (mt, g))
                nc.vector.tensor_tensor(result[:], y[mt, g][:], share[mt][:].rearrange("p v d -> p (v d)"), ALU.add)
                nc.sync.dma_start(out[mt * P : (mt + 1) * P, g * HL : (g + 1) * HL], result[:])
